import numpy as np
import ml_dtypes


def mxq(x, axis, fmt="e4m3"):
    dtype, down = {"e4m3": (ml_dtypes.float8_e4m3fn, 7), "e5m2": (ml_dtypes.float8_e5m2, 14)}[fmt]
    v = np.moveaxis(np.asarray(x, np.float32).astype(ml_dtypes.bfloat16).astype(np.float64), axis, -1)
    blocks = v.reshape(v.shape[:-1] + (-1, 32))
    amax = np.abs(blocks).max(-1, keepdims=True)
    byte = np.maximum(np.where(amax > 0, np.frexp(amax)[1] - 1 + 127, 0) - down, 1)
    scale = np.exp2(byte - 127.0)
    codes = (blocks / scale).astype(np.float32).astype(dtype).astype(np.float64)
    return np.moveaxis((codes * scale).reshape(v.shape), -1, axis)


WIDE = False


def mx_kscale(k):
    if not WIDE:
        return np.ones(k)
    levels = np.array([10, -10, 5, -5, 0])
    if k % 512:
        return np.exp2(np.random.permutation(np.resize(levels, k // 32))).repeat(32)
    a = np.empty((k // 512, 16))
    for p in range(k // 512):
        a[p, :8] = np.random.permutation(np.resize(levels, 8))
        for g in range(8):
            far = levels[np.abs(levels - a[p, g]) >= 10]
            a[p, g + 8] = far[np.random.randint(len(far))]
    return np.exp2(a.ravel()).repeat(32)


def f64(x):
    return np.asarray(x).astype(np.float64)


def striped(idx):
    return np.tile(idx.reshape(-1, 16).T, (8, 1)).astype(np.uint16)


def unstriped(offs):
    return offs[:16].T.reshape(-1).astype(np.int64)


def pack_weight(w):
    k, n = w.shape
    w = f64(np.asarray(w, np.float32).astype(ml_dtypes.bfloat16)).reshape(k // 32, 32, n)
    amax = np.abs(w).max(1)
    byte = np.clip(np.where(amax > 0, np.frexp(amax)[1] - 1 + 127 - 7, 1), 1, 254)
    scaled = (w * np.exp2(127.0 - byte)[:, None, :]).reshape(k, n).astype(np.float32)
    words = np.ascontiguousarray(scaled.reshape(k // 512, 128, 4, n).transpose(0, 1, 3, 2)).astype(ml_dtypes.float8_e4m3fn).view(np.uint8)
    return words, np.ascontiguousarray(byte.astype(np.uint8).reshape(k // 512, 16, n))


def unpack_weight(words, scales):
    g, p, n, _ = words.shape
    vals = np.ascontiguousarray(words).view(ml_dtypes.float8_e4m3fn).astype(np.float64) * np.repeat(np.exp2(scales.astype(np.float64) - 127.0), 8, axis=1)[..., None]
    return vals.transpose(0, 1, 3, 2).reshape(g * 512, n)


E2M1 = np.array([0.0, 0.5, 1.0, 1.5, 2.0, 3.0, 4.0, 6.0, -0.0, -0.5, -1.0, -1.5, -2.0, -3.0, -4.0, -6.0])


def pack_fp4(w):
    k, n = w.shape
    w = f64(np.asarray(w, np.float32).astype(ml_dtypes.bfloat16)).reshape(k // 32, 32, n)
    amax = np.abs(w).max(1)
    mant, ex = np.frexp(amax / 6.0)
    byte = np.clip(np.where(amax > 0, np.where(mant > 0.5, ex, ex - 1) + 127, 1), 1, 254)
    scaled = (w * np.exp2(127.0 - byte)[:, None, :]).reshape(k, n).astype(np.float32)
    c = np.ascontiguousarray(scaled.reshape(k // 512, 128, 4, n).transpose(0, 1, 3, 2)).astype(ml_dtypes.float4_e2m1fn).view(np.uint8) & 0xF
    words = (c[..., 0::2] | (c[..., 1::2] << 4)).reshape(k // 512, 128, 2 * n)
    return np.ascontiguousarray(words), np.ascontiguousarray(byte.astype(np.uint8).reshape(k // 512, 16, n))


def unpack_fp4(words, scales):
    g, _, n = scales.shape
    words = np.ascontiguousarray(words).reshape(g, 128, n, 2)
    nib = np.empty((g, 128, n, 4), np.uint8)
    nib[..., 0::2] = words & 0xF
    nib[..., 1::2] = words >> 4
    vals = E2M1[nib] * np.repeat(np.exp2(scales.astype(np.float64) - 127.0), 8, axis=1)[..., None]
    return vals.transpose(0, 1, 3, 2).reshape(g * 512, n)


K, T, S, N, H = 512, 2048, 512, 256, 512


def setup_inputs():
    n = np.random.standard_normal
    s = mx_kscale(K)[:, None]
    u = mx_kscale(H)
    packed_xT = pack_weight(n((K, T)) * s)
    packed_w1 = pack_fp4(n((K, H)) / np.sqrt(K) / s)
    packed_w2 = pack_fp4(n((K, H)) / np.sqrt(K) / s)
    packed_w3 = pack_fp4(n((H, N)) / np.sqrt(H) / u[:, None])
    return {
        "x_words": packed_xT[0],
        "x_scales": packed_xT[1],
        "w1_words": packed_w1[0],
        "w1_scales": packed_w1[1],
        "w2_words": packed_w2[0],
        "w2_scales": packed_w2[1],
        "unit": (np.random.uniform(0.6, 1.4, (H, 1)) * u[:, None]).astype(np.float32),
        "w3_words": packed_w3[0],
        "w3_scales": packed_w3[1],
        "offs": striped(np.random.permutation(T)[:S]),
        "ea": striped(np.random.permutation(S)),
        "eb": striped(np.random.permutation(S)),
    }


def reference(x_words, x_scales, w1_words, w1_scales, w2_words, w2_scales, unit, w3_words, w3_scales, offs, ea, eb):
    xq = unpack_weight(x_words, x_scales)[:, unstriped(offs)]
    qs = unpack_fp4(w1_words, w1_scales).T @ xq
    qv = unpack_fp4(w2_words, w2_scales).T @ xq
    nrm = np.sqrt((qs) ** 2 + (qv) ** 2 + 0.1)
    us = qs / nrm
    sa = us[:, unstriped(ea)]
    sb = us[:, unstriped(eb)]
    ut = qv / nrm
    ta = ut[:, unstriped(ea)]
    tb = ut[:, unstriped(eb)]
    cs = sa * sb - (ta * tb)
    ct = sa * tb + ta * sb
    err = -1.0 * (cs * us + ct * ut) + 1.0
    wgt = np.exp(-1.2 * err)
    hid = f64(unit) * (wgt - (0.3 * ((err) ** 2)))
    return unpack_fp4(w3_words, w3_scales).T @ mxq(hid, 0, "e4m3")

@@ -1,0 +1,226 @@
+import math
+from contextlib import ExitStack
+
+import concourse.mybir as mybir
+from concourse.masks import make_identity
+
+K, T, S, N, H = 512, 2048, 512, 256, 512
+FLOPS = 2 * K * H * S * 2 + 2 * H * N * S
+
+F32 = mybir.dt.float32
+BF16 = mybir.dt.bfloat16
+I32 = mybir.dt.int32
+U32 = mybir.dt.uint32
+U16 = mybir.dt.uint16
+U8 = mybir.dt.uint8
+FP8X4 = mybir.dt.float8_e4m3fn_x4
+FP4X4 = mybir.dt.float4_e2m1fn_x4
+ALU = mybir.AluOpType
+ACT = mybir.ActivationFunctionType
+
+P = 128
+PACK = 4
+ROW_TILES = H // P
+HALF = S // 2
+
+
+def load_scale_rows(queue, plane, scales):
+    for q in range(4):
+        queue.dma_start(plane[32 * q : 32 * q + 4, :].bitcast(I32), scales[0, 4 * q : 4 * q + 4, :].bitcast(I32))
+
+
+def tile_picked_ycycav_wgt_p_kernel(
+    tc, x_words, x_scales, w1_words, w1_scales, w2_words, w2_scales, unit, w3_words, w3_scales, offs, ea, eb, out
+):
+    nc = tc.nc
+    with ExitStack() as ctx:
+        keep = ctx.enter_context(tc.tile_pool(name="keep", bufs=1))
+        work = ctx.enter_context(tc.tile_pool(name="work", bufs=4))
+        psum = ctx.enter_context(tc.psum_pool(name="psum", bufs=8))
+
+        offs_t = keep.tile([P, S // 16], U16)
+        ea_t = keep.tile([P, S // 16], U16)
+        eb_t = keep.tile([P, S // 16], U16)
+        x_table = keep.tile([P, T], I32, align_bytes=64)
+        x_scale_table = keep.tile([P, T], U8, align_bytes=64)
+        w1_t = keep.tile([P, 2 * H], U8, align_bytes=64)
+        w2_t = keep.tile([P, 2 * H], U8, align_bytes=64)
+        w3_t = keep.tile([P, 2 * N], U8, align_bytes=64)
+        w1_plane = keep.tile([P, H], U8, align_bytes=64)
+        w2_plane = keep.tile([P, H], U8, align_bytes=64)
+        w3_plane = keep.tile([P, N], U8, align_bytes=64)
+        unit_t = keep.tile([P, PACK], F32)
+        gain = keep.tile([P, PACK], F32)
+        ident = keep.tile([P, P], F32)
+
+        nc.vector.memset(x_scale_table[:].bitcast(I32), 0)
+        nc.vector.memset(w1_plane[:].bitcast(I32), 0)
+        nc.vector.memset(w2_plane[:].bitcast(I32), 0)
+        nc.vector.memset(w3_plane[:].bitcast(I32), 0)
+
+        nc.sync.dma_start(offs_t[:], offs)
+        load_scale_rows(nc.sync, x_scale_table, x_scales)
+        nc.sync.dma_start(x_table[:], x_words[0].rearrange("p c r -> p (c r)").bitcast(I32))
+        nc.sync.dma_start(w1_t[:].bitcast(I32), w1_words[0].bitcast(I32))
+        nc.sync.dma_start(w2_t[:].bitcast(I32), w2_words[0].bitcast(I32))
+        load_scale_rows(nc.gpsimd, w2_plane, w2_scales)
+        load_scale_rows(nc.sync, w1_plane, w1_scales)
+        nc.sync.dma_start(eb_t[:], eb)
+        nc.sync.dma_start(ea_t[:], ea)
+        nc.sync.dma_start(unit_t[:], unit.rearrange("(p t) o -> p (t o)", t=PACK))
+        nc.sync.dma_start(w3_t[:].bitcast(I32), w3_words[0].bitcast(I32))
+        load_scale_rows(nc.sync, w3_plane, w3_scales)
+        make_identity(nc, ident[:])
+
+        x_codes = keep.tile([P, S], U32, align_bytes=64)
+        x_plane = keep.tile([P, S], U8, align_bytes=64)
+        nc.vector.tensor_copy(x_plane[:], x_scale_table[:].indirect(offs_t[:]))
+        nc.vector.tensor_copy(x_codes[:], x_table[:].bitcast(U32).indirect(offs_t[:]))
+        nc.vector.tensor_scalar(gain[:], unit_t[:], math.exp(-1.2), None, ALU.mult)
+
+        planes = [keep.tile([P, 3, S], F32, name=f"planes{b}") for b in range(ROW_TILES)]
+        q_banks = {}
+        norm2 = {}
+
+        def products(b):
+            squares = work.tile([P, 2, S], F32)
+            for c, (w_t, w_plane) in enumerate(((w1_t, w1_plane), (w2_t, w2_plane))):
+                q_banks[b, c] = psum.tile([P, S], F32, tag="bank", name="q_bank")
+                nc.tensor.matmul_mx(
+                    out=q_banks[b, c][:],
+                    lhsT=w_t[:, 2 * P * b : 2 * P * (b + 1)].bitcast(FP4X4),
+                    lhsT_scale=w_plane[:, P * b : P * (b + 1)],
+                    rhs=x_codes[:].bitcast(FP8X4),
+                    rhs_scale=x_plane[:],
+                    start=True,
+                    stop=True,
+                )
+                nc.scalar.activation(squares[:, c, :], q_banks[b, c][:], ACT.Square)
+            norm2[b] = work.tile([P, S], F32, name="norm2")
+            nc.vector.scalar_tensor_tensor(norm2[b][:], squares[:, 0, :], 0.1, squares[:, 1, :], ALU.add, ALU.add)
+
+        def normalise(b):
+            nc.scalar.activation(planes[b][:, 2, :], norm2[b][:], ACT.Abs_reciprocal_sqrt)
+            for c in range(2):
+                nc.vector.tensor_tensor(planes[b][:, c, :], q_banks[b, c][:], planes[b][:, 2, :], ALU.mult)
+
+        def fetch(name, lst, b, j0, w):
+            picked = work.tile([P, 2, w], F32, name=name, bufs=5)
+            for c in range(2):
+                window = planes[b][:, c : c + 2, :].rearrange("p c j -> p (c j)")
+                nc.scalar.activation(picked[:, c, :], window.indirect(lst[:, j0 // 16 : (j0 + w) // 16]), ACT.Copy)
+            return picked
+
+        def relate(zb, b, j0, w):
+            like = work.tile([P, 2, w], F32)
+            cross = work.tile([P, 2, w], F32)
+            rel = work.tile([P, 2, w], F32)
+            nc.vector.tensor_tensor(like[:], zb[:], planes[b][:, 0:2, j0 : j0 + w], ALU.mult)
+            for c in range(2):
+                nc.vector.tensor_tensor(cross[:, c, :], zb[:, c, :], planes[b][:, 1 - c, j0 : j0 + w], ALU.mult)
+            nc.vector.tensor_tensor(rel[:, 0, :], like[:, 0, :], like[:, 1, :], ALU.add)
+            nc.vector.tensor_tensor(rel[:, 1, :], cross[:, 0, :], cross[:, 1, :], ALU.subtract)
+            return rel
+
+        agree = {}
+
+        def compose(za, rel, b, j0, w):
+            terms = work.tile([P, 2, w], F32)
+            nc.vector.tensor_tensor(terms[:], za[:], rel[:], ALU.mult)
+            for jj in range(0, w, P):
+                jb = (j0 + jj) // P
+                if jb not in agree:
+                    agree[jb] = psum.tile([P, H], F32, tag="bank", name="agree")
+                for c in range(2):
+                    nc.tensor.matmul(
+                        agree[jb][:, P * b : P * (b + 1)],
+                        lhsT=terms[:, c, jj : jj + P],
+                        rhs=ident[:],
+                        is_transpose=True,
+                        start=(c == 0),
+                        stop=(c == 1),
+                    )
+
+        hid = keep.tile([P, S, PACK], BF16, align_bytes=64)
+
+        def weigh(jb):
+            dealt = agree[jb][:].rearrange("j (p t) -> j t p", t=PACK)
+            growth = work.tile([P, PACK, P], F32)
+            err2 = work.tile([P, PACK, P], F32)
+            nc.scalar.activation(growth[:], dealt, ACT.Exp, scale=1.2)
+            nc.scalar.activation(err2[:], dealt, ACT.Square, bias=1.0, scale=-1.0)
+            diff = work.tile([P, PACK, P], F32)
+            nc.vector.scalar_tensor_tensor(
+                diff[:].rearrange("j t p -> j (t p)"),
+                err2[:].rearrange("j t p -> j (t p)"),
+                -0.3 * math.exp(1.2),
+                growth[:].rearrange("j t p -> j (t p)"),
+                ALU.mult,
+                ALU.add,
+            )
+            back = psum.tile([P, PACK, P], F32, tag="bank", name="back")
+            for t in range(PACK):
+                nc.tensor.transpose(back[:, t, :], diff[:, t, :], ident[:])
+            nc.vector.tensor_tensor(
+                hid[:, P * jb : P * (jb + 1), :],
+                back[:].rearrange("p t j -> p j t"),
+                gain[:].unsqueeze(1).to_broadcast([P, P, PACK]),
+                ALU.mult,
+            )
+
+        out_v = out.rearrange("(h p) j -> p h j", p=P)
+
+        def view(j0, w):
+            hid_codes = work.tile([P, w], U32, align_bytes=64)
+            hid_plane = work.tile([P, w], U8, align_bytes=64)
+            nc.vector.quantize_mx(
+                out=hid_codes[:].bitcast(FP8X4),
+                scales=hid_plane[:],
+                in_=hid[:, j0 : j0 + w, :].rearrange("p j t -> p (j t)"),
+            )
+            views = psum.tile([P, N // P, w], F32, tag="bank", name="views")
+            for h in range(N // P):
+                nc.tensor.matmul_mx(
+                    out=views[:, h, :],
+                    lhsT=w3_t[:, 2 * P * h : 2 * P * (h + 1)].bitcast(FP4X4),
+                    lhsT_scale=w3_plane[:, P * h : P * (h + 1)],
+                    rhs=hid_codes[:].bitcast(FP8X4),
+                    rhs_scale=hid_plane[:],
+                    start=True,
+                    stop=True,
+                )
+            result = work.tile([P, N // P, w], F32)
+            nc.scalar.copy(result[:], views[:])
+            nc.sync.dma_start(out_v[:, :, j0 : j0 + w], result[:])
+
+        products(0)
+        for b in range(ROW_TILES):
+            if b + 1 < ROW_TILES:
+                products(b + 1)
+            normalise(b)
+
+        last = ROW_TILES - 1
+        pieces = [(b, 0, S) for b in range(last)] + [(last, 0, HALF), (last, HALF, HALF)]
+        zb = {}
+        za = {}
+        zb[0] = fetch("zb", eb_t, *pieces[0])
+        for k in range(3):
+            zb[k + 1] = fetch("zb", eb_t, *pieces[k + 1])
+            za[k] = fetch("za", ea_t, *pieces[k])
+        za[3] = fetch("za", ea_t, *pieces[3])
+        zb[4] = fetch("zb", eb_t, *pieces[4])
+        za[4] = fetch("za", ea_t, *pieces[4])
+
+        rel = {0: relate(zb[0], *pieces[0])}
+        for k in range(3):
+            rel[k + 1] = relate(zb[k + 1], *pieces[k + 1])
+            compose(za[k], rel[k], *pieces[k])
+        compose(za[3], rel[3], *pieces[3])
+        rel[4] = relate(zb[4], *pieces[4])
+        compose(za[4], rel[4], *pieces[4])
+
+        for jb in range(S // P):
+            weigh(jb)
+        view(0, HALF)
+        view(HALF, P)
+        view(HALF + P, P)

@@ -24,9 +24,9 @@ ROW_TILES = H // P
 HALF = S // 2
 
 
-def load_scale_rows(queue, plane, scales):
-    for q in range(4):
-        queue.dma_start(plane[32 * q : 32 * q + 4, :].bitcast(I32), scales[0, 4 * q : 4 * q + 4, :].bitcast(I32))
+def load_scale_rows(queue, plane, scales, quadrants):
+    for q in quadrants:
+        queue.dma_start(plane[32 * q : 32 * q + 4, :].bitcast(I32), scales[4 * q : 4 * q + 4, :].bitcast(I32))
 
 
 def tile_picked_ycycav_wgt_p_kernel(
@@ -43,70 +43,78 @@ def tile_picked_ycycav_wgt_p_kernel(
         eb_t = keep.tile([P, S // 16], U16)
         x_table = keep.tile([P, T], I32, align_bytes=64)
         x_scale_table = keep.tile([P, T], U8, align_bytes=64)
-        w1_t = keep.tile([P, 2 * H], U8, align_bytes=64)
-        w2_t = keep.tile([P, 2 * H], U8, align_bytes=64)
-        w3_t = keep.tile([P, 2 * N], U8, align_bytes=64)
-        w1_plane = keep.tile([P, H], U8, align_bytes=64)
-        w2_plane = keep.tile([P, H], U8, align_bytes=64)
-        w3_plane = keep.tile([P, N], U8, align_bytes=64)
-        unit_t = keep.tile([P, PACK], F32)
+        w1_t = keep.tile([P, 2 * H], U8, align_bytes=64, tag="w1_then_w3")
+        w2_t = keep.tile([P, 2 * H], U8, align_bytes=64, tag="w2_then_unit")
+        w_planes = keep.tile([P, 2 * H], U8, align_bytes=64)
+        w1_plane = w_planes[:, 0:H]
+        w2_plane = w_planes[:, H : 2 * H]
         gain = keep.tile([P, PACK], F32)
         ident = keep.tile([P, P], F32)
 
-        nc.vector.memset(x_scale_table[:].bitcast(I32), 0)
-        nc.vector.memset(w1_plane[:].bitcast(I32), 0)
-        nc.vector.memset(w2_plane[:].bitcast(I32), 0)
-        nc.vector.memset(w3_plane[:].bitcast(I32), 0)
+        w_rows = keep.tile([16, 2 * H], U8)
 
+        nc.gpsimd.memset(x_scale_table[:].bitcast(I32), 0)
+        nc.gpsimd.dma_start(w2_t[:].bitcast(I32), w2_words[0].bitcast(I32))
+        nc.vector.memset(w_planes[:].bitcast(I32), 0)
+
+        nc.sync.dma_start(w_rows[:, 0:H].bitcast(I32), w1_scales[0].bitcast(I32))
+        nc.sync.dma_start(w_rows[:, H : 2 * H].bitcast(I32), w2_scales[0].bitcast(I32))
         nc.sync.dma_start(offs_t[:], offs)
-        load_scale_rows(nc.sync, x_scale_table, x_scales)
+        load_scale_rows(nc.sync, x_scale_table, x_scales[0], range(4))
         nc.sync.dma_start(x_table[:], x_words[0].rearrange("p c r -> p (c r)").bitcast(I32))
         nc.sync.dma_start(w1_t[:].bitcast(I32), w1_words[0].bitcast(I32))
-        nc.sync.dma_start(w2_t[:].bitcast(I32), w2_words[0].bitcast(I32))
-        load_scale_rows(nc.gpsimd, w2_plane, w2_scales)
-        load_scale_rows(nc.sync, w1_plane, w1_scales)
         nc.sync.dma_start(eb_t[:], eb)
         nc.sync.dma_start(ea_t[:], ea)
-        nc.sync.dma_start(unit_t[:], unit.rearrange("(p t) o -> p (t o)", t=PACK))
-        nc.sync.dma_start(w3_t[:].bitcast(I32), w3_words[0].bitcast(I32))
-        load_scale_rows(nc.sync, w3_plane, w3_scales)
+        load_scale_rows(nc.scalar, w_planes, w_rows, range(4))
         make_identity(nc, ident[:])
 
-        x_codes = keep.tile([P, S], U32, align_bytes=64)
-        x_plane = keep.tile([P, S], U8, align_bytes=64)
-        nc.vector.tensor_copy(x_plane[:], x_scale_table[:].indirect(offs_t[:]))
-        nc.vector.tensor_copy(x_codes[:], x_table[:].bitcast(U32).indirect(offs_t[:]))
-        nc.vector.tensor_scalar(gain[:], unit_t[:], math.exp(-1.2), None, ALU.mult)
+        x_codes = [keep.tile([P, HALF], U32, align_bytes=64, name=f"x_codes{half}") for half in range(2)]
+        x_plane = [keep.tile([P, HALF], U8, align_bytes=64, name=f"x_plane{half}", tag=f"plane{half}") for half in range(2)]
+        for half in range(2):
+            entries = offs_t[:, half * HALF // 16 : (half + 1) * HALF // 16]
+            nc.vector.tensor_copy(x_plane[half][:], x_scale_table[:].indirect(entries))
+            nc.vector.tensor_copy(x_codes[half][:], x_table[:].bitcast(U32).indirect(entries))
 
         planes = [keep.tile([P, 3, S], F32, name=f"planes{b}") for b in range(ROW_TILES)]
         q_banks = {}
         norm2 = {}
 
-        def products(b):
-            squares = work.tile([P, 2, S], F32)
+        squares = [work.tile([P, 2, 2, HALF], F32, name="squares") for b in range(ROW_TILES)]
+
+        def products(b, half):
+            q_banks[b, half] = psum.tile([P, 2, HALF], F32, tag="bank", name="q_bank")
             for c, (w_t, w_plane) in enumerate(((w1_t, w1_plane), (w2_t, w2_plane))):
-                q_banks[b, c] = psum.tile([P, S], F32, tag="bank", name="q_bank")
                 nc.tensor.matmul_mx(
-                    out=q_banks[b, c][:],
+                    out=q_banks[b, half][:, c, :],
                     lhsT=w_t[:, 2 * P * b : 2 * P * (b + 1)].bitcast(FP4X4),
                     lhsT_scale=w_plane[:, P * b : P * (b + 1)],
-                    rhs=x_codes[:].bitcast(FP8X4),
-                    rhs_scale=x_plane[:],
+                    rhs=x_codes[half][:].bitcast(FP8X4),
+                    rhs_scale=x_plane[half][:],
                     start=True,
                     stop=True,
                 )
-                nc.scalar.activation(squares[:, c, :], q_banks[b, c][:], ACT.Square)
-            norm2[b] = work.tile([P, S], F32, name="norm2")
-            nc.vector.scalar_tensor_tensor(norm2[b][:], squares[:, 0, :], 0.1, squares[:, 1, :], ALU.add, ALU.add)
+            nc.scalar.activation(squares[b][:, half], q_banks[b, half][:], ACT.Square)
+
+        def add_squares(b):
+            norm2[b] = work.tile([P, 2, HALF], F32, name="norm2")
+            nc.vector.scalar_tensor_tensor(
+                norm2[b][:], squares[b][:, :, 0, :], 0.1, squares[b][:, :, 1, :], ALU.add, ALU.add
+            )
 
         def normalise(b):
-            nc.scalar.activation(planes[b][:, 2, :], norm2[b][:], ACT.Abs_reciprocal_sqrt)
-            for c in range(2):
-                nc.vector.tensor_tensor(planes[b][:, c, :], q_banks[b, c][:], planes[b][:, 2, :], ALU.mult)
+            nc.scalar.activation(planes[b][:, 2, :], norm2[b][:].rearrange("p h j -> p (h j)"), ACT.Abs_reciprocal_sqrt)
+            for half in range(2):
+                cols = slice(half * HALF, (half + 1) * HALF)
+                nc.vector.tensor_tensor(
+                    planes[b][:, 0:2, cols],
+                    q_banks[b, half][:],
+                    planes[b][:, 2:3, cols].to_broadcast([P, 2, HALF]),
+                    ALU.mult,
+                )
 
-        def fetch(name, lst, b, j0, w):
+        def fetch(name, lst, b, j0, w, first=0):
             picked = work.tile([P, 2, w], F32, name=name, bufs=5)
-            for c in range(2):
+            for c in range(first, 2):
                 window = planes[b][:, c : c + 2, :].rearrange("p c j -> p (c j)")
                 nc.scalar.activation(picked[:, c, :], window.indirect(lst[:, j0 // 16 : (j0 + w) // 16]), ACT.Copy)
             return picked
@@ -126,7 +134,13 @@ def tile_picked_ycycav_wgt_p_kernel(
 
         def compose(za, rel, b, j0, w):
             terms = work.tile([P, 2, w], F32)
-            nc.vector.tensor_tensor(terms[:], za[:], rel[:], ALU.mult)
+            if b < ROW_TILES - 1:
+                nc.vector.tensor_tensor(terms[:], za[:], rel[:], ALU.mult)
+            else:
+                window = planes[b][:].rearrange("p c j -> p (c j)")
+                entries = ea_t[:, j0 // 16 : (j0 + w) // 16]
+                nc.vector.tensor_tensor(terms[:, 0, :], window.indirect(entries), rel[:, 0, :], ALU.mult)
+                nc.vector.tensor_tensor(terms[:, 1, :], za[:, 1, :], rel[:, 1, :], ALU.mult)
             for jj in range(0, w, P):
                 jb = (j0 + jj) // P
                 if jb not in agree:
@@ -143,24 +157,24 @@ def tile_picked_ycycav_wgt_p_kernel(
 
         hid = keep.tile([P, S, PACK], BF16, align_bytes=64)
 
-        def weigh(jb):
+        def weigh(jb, step):
             dealt = agree[jb][:].rearrange("j (p t) -> j t p", t=PACK)
-            growth = work.tile([P, PACK, P], F32)
-            err2 = work.tile([P, PACK, P], F32)
-            nc.scalar.activation(growth[:], dealt, ACT.Exp, scale=1.2)
-            nc.scalar.activation(err2[:], dealt, ACT.Square, bias=1.0, scale=-1.0)
-            diff = work.tile([P, PACK, P], F32)
-            nc.vector.scalar_tensor_tensor(
-                diff[:].rearrange("j t p -> j (t p)"),
-                err2[:].rearrange("j t p -> j (t p)"),
-                -0.3 * math.exp(1.2),
-                growth[:].rearrange("j t p -> j (t p)"),
-                ALU.mult,
-                ALU.add,
-            )
+            growth = work.tile([P, PACK * P], F32)
+            err2 = work.tile([P, PACK * P], F32)
+            diff = work.tile([P, PACK * P], F32)
             back = psum.tile([P, PACK, P], F32, tag="bank", name="back")
-            for t in range(PACK):
-                nc.tensor.transpose(back[:, t, :], diff[:, t, :], ident[:])
+            for t0 in range(0, PACK, step):
+                cols = slice(t0 * P, (t0 + step) * P)
+                src = dealt[:, t0 : t0 + step, :]
+                nc.scalar.activation(growth[:, cols].rearrange("j (t p) -> j t p", p=P), src, ACT.Exp, scale=1.2)
+                nc.scalar.activation(
+                    err2[:, cols].rearrange("j (t p) -> j t p", p=P), src, ACT.Square, bias=1.0, scale=-1.0
+                )
+                nc.vector.scalar_tensor_tensor(
+                    diff[:, cols], err2[:, cols], -0.3 * math.exp(1.2), growth[:, cols], ALU.mult, ALU.add
+                )
+                for t in range(t0, t0 + step):
+                    nc.tensor.transpose(back[:, t, :], diff[:, t * P : (t + 1) * P], ident[:])
             nc.vector.tensor_tensor(
                 hid[:, P * jb : P * (jb + 1), :],
                 back[:].rearrange("p t j -> p j t"),
@@ -193,11 +207,27 @@ def tile_picked_ycycav_wgt_p_kernel(
             nc.scalar.copy(result[:], views[:])
             nc.sync.dma_start(out_v[:, :, j0 : j0 + w], result[:])
 
-        products(0)
-        for b in range(ROW_TILES):
-            if b + 1 < ROW_TILES:
-                products(b + 1)
-            normalise(b)
+        for half in range(2):
+            for b in range(2):
+                products(b, half)
+        add_squares(0)
+        add_squares(1)
+        normalise(0)
+        for b in range(2, ROW_TILES):
+            for half in range(2):
+                products(b, half)
+            add_squares(b)
+            normalise(b - 1)
+        normalise(ROW_TILES - 1)
+
+        w3_t = keep.tile([P, 2 * N], U8, align_bytes=64, tag="w1_then_w3")
+        nc.sync.dma_start(w3_t[:].bitcast(I32), w3_words[0].bitcast(I32))
+        w3_plane = keep.tile([P, N], U8, align_bytes=64, tag="plane0")
+        nc.gpsimd.memset(w3_plane[:].bitcast(I32), 0)
+        load_scale_rows(nc.sync, w3_plane, w3_scales[0], range(4))
+        unit_t = keep.tile([P, PACK], F32, align_bytes=64, tag="w2_then_unit")
+        nc.sync.dma_start(unit_t[:], unit.rearrange("(p t) o -> p (t o)", t=PACK))
+        nc.gpsimd.tensor_scalar(gain[:], unit_t[:], math.exp(-1.2), 0.0, ALU.mult, ALU.add)
 
         last = ROW_TILES - 1
         pieces = [(b, 0, S) for b in range(last)] + [(last, 0, HALF), (last, HALF, HALF)]
@@ -207,9 +237,9 @@ def tile_picked_ycycav_wgt_p_kernel(
         for k in range(3):
             zb[k + 1] = fetch("zb", eb_t, *pieces[k + 1])
             za[k] = fetch("za", ea_t, *pieces[k])
-        za[3] = fetch("za", ea_t, *pieces[3])
+        za[3] = fetch("za", ea_t, *pieces[3], first=1)
         zb[4] = fetch("zb", eb_t, *pieces[4])
-        za[4] = fetch("za", ea_t, *pieces[4])
+        za[4] = fetch("za", ea_t, *pieces[4], first=1)
 
         rel = {0: relate(zb[0], *pieces[0])}
         for k in range(3):
@@ -220,7 +250,7 @@ def tile_picked_ycycav_wgt_p_kernel(
         compose(za[4], rel[4], *pieces[4])
 
         for jb in range(S // P):
-            weigh(jb)
+            weigh(jb, PACK if jb < S // P - 1 else PACK // 2)
         view(0, HALF)
         view(HALF, P)
         view(HALF + P, P)

@@ -55,6 +55,9 @@ def tile_picked_ycycav_wgt_p_kernel(
 
         nc.gpsimd.memset(x_scale_table[:].bitcast(I32), 0)
         nc.gpsimd.dma_start(w2_t[:].bitcast(I32), w2_words[0].bitcast(I32))
+        warm = keep.tile([P, 2], F32)
+        nc.vector.memset(warm[:, 0:1], 1.0)
+        nc.scalar.activation(warm[:, 1:2], warm[:, 0:1], ACT.Abs_reciprocal_sqrt)
         nc.vector.memset(w_planes[:].bitcast(I32), 0)
 
         nc.sync.dma_start(w_rows[:, 0:H].bitcast(I32), w1_scales[0].bitcast(I32))

import math
from contextlib import ExitStack

import concourse.mybir as mybir
from concourse.masks import make_identity

K, T, S, N, H = 512, 2048, 512, 256, 512
FLOPS = 2 * K * H * S * 2 + 2 * H * N * S

F32 = mybir.dt.float32
BF16 = mybir.dt.bfloat16
I32 = mybir.dt.int32
U32 = mybir.dt.uint32
U16 = mybir.dt.uint16
U8 = mybir.dt.uint8
FP8X4 = mybir.dt.float8_e4m3fn_x4
FP4X4 = mybir.dt.float4_e2m1fn_x4
ALU = mybir.AluOpType
ACT = mybir.ActivationFunctionType

P = 128
PACK = 4
ROW_TILES = H // P
HALF = S // 2


def load_scale_rows(queue, plane, scales, quadrants):
    for q in quadrants:
        queue.dma_start(plane[32 * q : 32 * q + 4, :].bitcast(I32), scales[4 * q : 4 * q + 4, :].bitcast(I32))


def tile_picked_ycycav_wgt_p_kernel(
    tc, x_words, x_scales, w1_words, w1_scales, w2_words, w2_scales, unit, w3_words, w3_scales, offs, ea, eb, out
):
    nc = tc.nc
    with ExitStack() as ctx:
        keep = ctx.enter_context(tc.tile_pool(name="keep", bufs=1))
        work = ctx.enter_context(tc.tile_pool(name="work", bufs=4))
        psum = ctx.enter_context(tc.psum_pool(name="psum", bufs=8))

        offs_t = keep.tile([P, S // 16], U16)
        ea_t = keep.tile([P, S // 16], U16)
        eb_t = keep.tile([P, S // 16], U16)
        x_table = keep.tile([P, T], I32, align_bytes=64)
        x_scale_table = keep.tile([P, T], U8, align_bytes=64)
        w1_t = keep.tile([P, 2 * H], U8, align_bytes=64, tag="w1_then_w3")
        w2_t = keep.tile([P, 2 * H], U8, align_bytes=64, tag="w2_then_unit")
        w_planes = keep.tile([P, 2 * H], U8, align_bytes=64)
        w1_plane = w_planes[:, 0:H]
        w2_plane = w_planes[:, H : 2 * H]
        gain = keep.tile([P, PACK], F32)
        ident = keep.tile([P, P], F32)

        w_rows = keep.tile([16, 2 * H], U8)

        nc.gpsimd.memset(x_scale_table[:].bitcast(I32), 0)
        nc.gpsimd.dma_start(w2_t[:].bitcast(I32), w2_words[0].bitcast(I32))
        warm = keep.tile([P, 2], F32)
        nc.vector.memset(warm[:, 0:1], 1.0)
        nc.scalar.activation(warm[:, 1:2], warm[:, 0:1], ACT.Abs_reciprocal_sqrt)
        nc.vector.memset(w_planes[:].bitcast(I32), 0)

        nc.sync.dma_start(w_rows[:, 0:H].bitcast(I32), w1_scales[0].bitcast(I32))
        nc.sync.dma_start(w_rows[:, H : 2 * H].bitcast(I32), w2_scales[0].bitcast(I32))
        nc.sync.dma_start(offs_t[:], offs)
        load_scale_rows(nc.sync, x_scale_table, x_scales[0], range(4))
        nc.sync.dma_start(x_table[:], x_words[0].rearrange("p c r -> p (c r)").bitcast(I32))
        nc.sync.dma_start(w1_t[:].bitcast(I32), w1_words[0].bitcast(I32))
        nc.sync.dma_start(eb_t[:], eb)
        nc.sync.dma_start(ea_t[:], ea)
        load_scale_rows(nc.scalar, w_planes, w_rows, range(4))
        make_identity(nc, ident[:])

        x_codes = [keep.tile([P, HALF], U32, align_bytes=64, name=f"x_codes{half}") for half in range(2)]
        x_plane = [keep.tile([P, HALF], U8, align_bytes=64, name=f"x_plane{half}", tag=f"plane{half}") for half in range(2)]
        for half in range(2):
            entries = offs_t[:, half * HALF // 16 : (half + 1) * HALF // 16]
            nc.vector.tensor_copy(x_plane[half][:], x_scale_table[:].indirect(entries))
            nc.vector.tensor_copy(x_codes[half][:], x_table[:].bitcast(U32).indirect(entries))

        planes = [keep.tile([P, 3, S], F32, name=f"planes{b}") for b in range(ROW_TILES)]
        q_banks = {}
        norm2 = {}

        squares = [work.tile([P, 2, 2, HALF], F32, name="squares") for b in range(ROW_TILES)]

        def products(b, half):
            q_banks[b, half] = psum.tile([P, 2, HALF], F32, tag="bank", name="q_bank")
            for c, (w_t, w_plane) in enumerate(((w1_t, w1_plane), (w2_t, w2_plane))):
                nc.tensor.matmul_mx(
                    out=q_banks[b, half][:, c, :],
                    lhsT=w_t[:, 2 * P * b : 2 * P * (b + 1)].bitcast(FP4X4),
                    lhsT_scale=w_plane[:, P * b : P * (b + 1)],
                    rhs=x_codes[half][:].bitcast(FP8X4),
                    rhs_scale=x_plane[half][:],
                    start=True,
                    stop=True,
                )
            nc.scalar.activation(squares[b][:, half], q_banks[b, half][:], ACT.Square)

        def add_squares(b):
            norm2[b] = work.tile([P, 2, HALF], F32, name="norm2")
            nc.vector.scalar_tensor_tensor(
                norm2[b][:], squares[b][:, :, 0, :], 0.1, squares[b][:, :, 1, :], ALU.add, ALU.add
            )

        def normalise(b):
            nc.scalar.activation(planes[b][:, 2, :], norm2[b][:].rearrange("p h j -> p (h j)"), ACT.Abs_reciprocal_sqrt)
            for half in range(2):
                cols = slice(half * HALF, (half + 1) * HALF)
                nc.vector.tensor_tensor(
                    planes[b][:, 0:2, cols],
                    q_banks[b, half][:],
                    planes[b][:, 2:3, cols].to_broadcast([P, 2, HALF]),
                    ALU.mult,
                )

        def fetch(name, lst, b, j0, w, first=0):
            picked = work.tile([P, 2, w], F32, name=name, bufs=5)
            for c in range(first, 2):
                window = planes[b][:, c : c + 2, :].rearrange("p c j -> p (c j)")
                nc.scalar.activation(picked[:, c, :], window.indirect(lst[:, j0 // 16 : (j0 + w) // 16]), ACT.Copy)
            return picked

        def relate(zb, b, j0, w):
            like = work.tile([P, 2, w], F32)
            cross = work.tile([P, 2, w], F32)
            rel = work.tile([P, 2, w], F32)
            nc.vector.tensor_tensor(like[:], zb[:], planes[b][:, 0:2, j0 : j0 + w], ALU.mult)
            for c in range(2):
                nc.vector.tensor_tensor(cross[:, c, :], zb[:, c, :], planes[b][:, 1 - c, j0 : j0 + w], ALU.mult)
            nc.vector.tensor_tensor(rel[:, 0, :], like[:, 0, :], like[:, 1, :], ALU.add)
            nc.vector.tensor_tensor(rel[:, 1, :], cross[:, 0, :], cross[:, 1, :], ALU.subtract)
            return rel

        agree = {}

        def compose(za, rel, b, j0, w):
            terms = work.tile([P, 2, w], F32)
            if b < ROW_TILES - 1:
                nc.vector.tensor_tensor(terms[:], za[:], rel[:], ALU.mult)
            else:
                window = planes[b][:].rearrange("p c j -> p (c j)")
                entries = ea_t[:, j0 // 16 : (j0 + w) // 16]
                nc.vector.tensor_tensor(terms[:, 0, :], window.indirect(entries), rel[:, 0, :], ALU.mult)
                nc.vector.tensor_tensor(terms[:, 1, :], za[:, 1, :], rel[:, 1, :], ALU.mult)
            for jj in range(0, w, P):
                jb = (j0 + jj) // P
                if jb not in agree:
                    agree[jb] = psum.tile([P, H], F32, tag="bank", name="agree")
                for c in range(2):
                    nc.tensor.matmul(
                        agree[jb][:, P * b : P * (b + 1)],
                        lhsT=terms[:, c, jj : jj + P],
                        rhs=ident[:],
                        is_transpose=True,
                        start=(c == 0),
                        stop=(c == 1),
                    )

        hid = keep.tile([P, S, PACK], BF16, align_bytes=64)

        def weigh(jb, step):
            dealt = agree[jb][:].rearrange("j (p t) -> j t p", t=PACK)
            growth = work.tile([P, PACK * P], F32)
            err2 = work.tile([P, PACK * P], F32)
            diff = work.tile([P, PACK * P], F32)
            back = psum.tile([P, PACK, P], F32, tag="bank", name="back")
            for t0 in range(0, PACK, step):
                cols = slice(t0 * P, (t0 + step) * P)
                src = dealt[:, t0 : t0 + step, :]
                nc.scalar.activation(growth[:, cols].rearrange("j (t p) -> j t p", p=P), src, ACT.Exp, scale=1.2)
                nc.scalar.activation(
                    err2[:, cols].rearrange("j (t p) -> j t p", p=P), src, ACT.Square, bias=1.0, scale=-1.0
                )
                nc.vector.scalar_tensor_tensor(
                    diff[:, cols], err2[:, cols], -0.3 * math.exp(1.2), growth[:, cols], ALU.mult, ALU.add
                )
                for t in range(t0, t0 + step):
                    nc.tensor.transpose(back[:, t, :], diff[:, t * P : (t + 1) * P], ident[:])
            nc.vector.tensor_tensor(
                hid[:, P * jb : P * (jb + 1), :],
                back[:].rearrange("p t j -> p j t"),
                gain[:].unsqueeze(1).to_broadcast([P, P, PACK]),
                ALU.mult,
            )

        out_v = out.rearrange("(h p) j -> p h j", p=P)

        def view(j0, w):
            hid_codes = work.tile([P, w], U32, align_bytes=64)
            hid_plane = work.tile([P, w], U8, align_bytes=64)
            nc.vector.quantize_mx(
                out=hid_codes[:].bitcast(FP8X4),
                scales=hid_plane[:],
                in_=hid[:, j0 : j0 + w, :].rearrange("p j t -> p (j t)"),
            )
            views = psum.tile([P, N // P, w], F32, tag="bank", name="views")
            for h in range(N // P):
                nc.tensor.matmul_mx(
                    out=views[:, h, :],
                    lhsT=w3_t[:, 2 * P * h : 2 * P * (h + 1)].bitcast(FP4X4),
                    lhsT_scale=w3_plane[:, P * h : P * (h + 1)],
                    rhs=hid_codes[:].bitcast(FP8X4),
                    rhs_scale=hid_plane[:],
                    start=True,
                    stop=True,
                )
            result = work.tile([P, N // P, w], F32)
            nc.scalar.copy(result[:], views[:])
            nc.sync.dma_start(out_v[:, :, j0 : j0 + w], result[:])

        for half in range(2):
            for b in range(2):
                products(b, half)
        add_squares(0)
        add_squares(1)
        normalise(0)
        for b in range(2, ROW_TILES):
            for half in range(2):
                products(b, half)
            add_squares(b)
            normalise(b - 1)
        normalise(ROW_TILES - 1)

        w3_t = keep.tile([P, 2 * N], U8, align_bytes=64, tag="w1_then_w3")
        nc.sync.dma_start(w3_t[:].bitcast(I32), w3_words[0].bitcast(I32))
        w3_plane = keep.tile([P, N], U8, align_bytes=64, tag="plane0")
        nc.gpsimd.memset(w3_plane[:].bitcast(I32), 0)
        load_scale_rows(nc.sync, w3_plane, w3_scales[0], range(4))
        unit_t = keep.tile([P, PACK], F32, align_bytes=64, tag="w2_then_unit")
        nc.sync.dma_start(unit_t[:], unit.rearrange("(p t) o -> p (t o)", t=PACK))
        nc.gpsimd.tensor_scalar(gain[:], unit_t[:], math.exp(-1.2), 0.0, ALU.mult, ALU.add)

        last = ROW_TILES - 1
        pieces = [(b, 0, S) for b in range(last)] + [(last, 0, HALF), (last, HALF, HALF)]
        zb = {}
        za = {}
        zb[0] = fetch("zb", eb_t, *pieces[0])
        for k in range(3):
            zb[k + 1] = fetch("zb", eb_t, *pieces[k + 1])
            za[k] = fetch("za", ea_t, *pieces[k])
        za[3] = fetch("za", ea_t, *pieces[3], first=1)
        zb[4] = fetch("zb", eb_t, *pieces[4])
        za[4] = fetch("za", ea_t, *pieces[4], first=1)

        rel = {0: relate(zb[0], *pieces[0])}
        for k in range(3):
            rel[k + 1] = relate(zb[k + 1], *pieces[k + 1])
            compose(za[k], rel[k], *pieces[k])
        compose(za[3], rel[3], *pieces[3])
        rel[4] = relate(zb[4], *pieces[4])
        compose(za[4], rel[4], *pieces[4])

        for jb in range(S // P):
            weigh(jb, PACK if jb < S // P - 1 else PACK // 2)
        view(0, HALF)
        view(HALF, P)
        view(HALF + P, P)
